import numpy as np, ml_dtypes
CORES = [83,85,87,115,117,119]
N = 6
import mx_ref
NC, G = 128, 2
C, C2 = np.float32(0.043), np.float32(0.01755)
BF = ml_dtypes.bfloat16
def cut(t, i, w=512):
    return t[:, w * i:w * i + w]
def tile(rs):
    return np.stack(rs, axis=2).reshape(128, -1).astype(BF)
def layer(w, X):
    out = []
    for i in range(G):
        for t in range(len(X)):
            p = mx_ref.matmul(mx_ref.quantize(cut(w, len(X) * i + t)), X[t])
            z = p if t == 0 else z + p
        out.append(z)
    return out
def act(Z):
    return [np.maximum(s * z, 0) * C for z in Z for s in (1, -1)]
def act2(Z):
    return [np.maximum(s * z, 0) * C2 for z in Z for s in (1, -1)]
def setup_inputs(rng):
    def f(*shape):
        return mx_ref.flush((rng.standard_normal(shape, dtype=np.float32) * np.exp2(rng.integers(-2, 3, shape[:-1] + (1,)))).astype(BF))
    return {"x": f(N, 128, 4 * NC), "w1": f(N, 128, G * 512), "w2": f(N, 128, G * 512), "w3": f(N, 128, G * 512)}
def setup_inputs_blocks(rng):
    d = setup_inputs(rng)
    for k in ("x", "w1", "w2", "w3"): d[k] = mx_ref.spread(d[k], rng, 2)
    return d
def setup_inputs_wide(rng):
    d = setup_inputs(rng)
    for k in ("x", "w1", "w2", "w3"): d[k] = mx_ref.flush((d[k].astype(np.float32) * np.exp2(rng.integers(-4, 5, (N, 1, 1))).astype(np.float32)).astype(BF))
    return d
def reference(x, w1, w2, w3, own=None):
    X = [mx_ref.quantize(x[j]) for j in range(N)]
    t = np.stack([np.stack([tile(act(layer(w1[r], [X[c]]))) for c in range(N)]) for r in range(N)])
    uset = t if own is None else own["t"]
    h = np.zeros((N, 128, 4 * NC), BF)
    for c in range(N):
        for r in range(N):
            P = layer(w2[r], [mx_ref.quantize(uset[r][c])])
            Z = P if r == 0 else [z + p for z, p in zip(Z, P)]
        h[c] = tile(act2(Z))
    use = h if own is None else own["h"]
    H = [mx_ref.quantize(use[j]) for j in range(N)]
    y = np.zeros((N, 128, N * G * NC), np.float32)
    for r in range(N):
        for j in range(N):
            Z = layer(w3[r], [H[j]])
            for i in range(G):
                y[r][:, NC * (G * j + i):NC * (G * j + i) + NC] = Z[i]
    return {"t": t, "h": h, "y": y}

@@ -1,0 +1,282 @@
+import numpy as np
+from concourse.bass import DstId, RemoteDMATransfer
+from concourse.mybir import dt, AluOpType, ActivationFunctionType
+
+N = 6
+NC = 128
+C1 = float(np.float32(0.043))
+C2 = float(np.float32(0.01755))
+CODES = "float8_e4m3fn_x4"
+OPT = {"x": "fwd", "h": "fwd"}
+
+
+def packed(name, n):
+    return {name + "q": ("sbuf", [128, n], CODES), name + "s": ("sbuf", [128, n], "uint8")}
+
+
+SCRATCH = {
+    "xb": ("sbuf", [128, 4 * NC], "bfloat16"),
+    "wb1": ("sbuf", [128, 1024], "bfloat16"),
+    "wb2": ("sbuf", [128, 1024], "bfloat16"),
+    "wb3": ("sbuf", [128, 1024], "bfloat16"),
+    "tt": ("sbuf", [128, N * 4 * NC], "bfloat16"),
+    "ht": ("sbuf", [128, 4 * NC], "bfloat16"),
+    "rb": ("sbuf", [128, 256], "float32"),
+    "pc": ("sbuf", [128, 256], "float32"),
+    "sf": ("sbuf", [128, 256], "float32"),
+    "yb": ("sbuf", [128, N * 256], "float32"),
+    "ps": ("psum", [128, 512 * 8], "float32"),
+}
+SCRATCH.update(packed("w1", 256))
+SCRATCH.update(packed("w2", 256))
+SCRATCH.update(packed("w3", 256))
+SCRATCH.update(packed("wp", 512))
+SCRATCH.update(packed("x", N * NC))
+SCRATCH.update(packed("t", N * NC))
+SCRATCH.update(packed("u", 4 * NC))
+SCRATCH.update(packed("h", N * NC))
+
+SEMAPHORES = (["ldx", "ldw1", "ldw2", "ldw3", "qx", "qw1", "qw2", "qw3", "sent", "sentm", "sentv", "sentc", "stored",
+               "own", "rb", "pc", "sf0", "sf1", "sT", "hA", "hV", "qh"]
+              + ["%s%s%d" % (n, e, r) for n in "xhwuv" for e in "qs" for r in range(N)]
+              + ["%s%d" % (n, s) for n in ("za", "zb", "tA", "tV", "qt", "ya", "yv", "yc") for s in range(N)])
+
+
+def rank_program(g, core, T, topo):
+    rank = T.rank_of(core)
+    if rank is None:
+        return
+    S = T.sem
+    cores = T.cores
+
+    def home(r):
+        return [q for q in range(N) if topo.chip(cores[q]) == topo.chip(cores[r])]
+
+    def twin(r):
+        away = [q for q in range(N) if topo.chip(cores[q]) != topo.chip(cores[r])]
+        return away[home(r).index(r)]
+
+    def peers(r):
+        h = home(r)
+        k = h.index(r)
+        return [h[(k + d) % len(h)] for d in range(1, len(h))]
+
+    def slots(r):
+        out = []
+        for q in [r] + peers(r):
+            out += [q, twin(q)]
+        return out
+
+    def dst(r):
+        rid, pid, _ = topo.addr(cores[r])
+        return DstId(rid=rid, pnc=pid)
+
+    def bits(m):
+        return [e for e in range(16) if (m >> e) & 1]
+
+    me, pe, tw = slots(rank), peers(rank), twin(rank)
+    away = [r for r in range(N) if r not in home(rank)]
+    far = topo.mask(core, cores[tw])
+    near = topo.mask(core, cores[pe[0]])
+    rest = near & ~far
+    nb = bits(near)
+    split = [sum(1 << e for e in nb[0::2]), sum(1 << e for e in nb[1::2])]
+    n_far, n_rest, n_split = len(bits(far)), len(bits(rest)), len(bits(split[0]))
+    sent = {}
+
+    def col(s, w=NC, n=1):
+        return slice(w * s, w * (s + n))
+
+    def raw(name, e, sl):
+        v = T[name + e][:, sl]
+        return v.bitcast(dt.uint8) if e == "q" else v
+
+    def bank(b):
+        return T.ps[:, 512 * b:512 * b + NC]
+
+    def copy(src, dsts, mask, sem):
+        return RemoteDMATransfer(dst_ids=[dst(d) for d, _ in dsts], dma_engine_mask=mask, remote_sem=S[sem],
+                                 srcs=[src], dsts=[a for _, a in dsts], alu_op=0)
+
+    def call(transfers, n, sem="sent"):
+        g.remote_dma_fused(transfers, local_sem=S[sem])
+        sent[sem] = sent.get(sem, 0) + n
+
+    def slot_of(d, r):
+        return slots(d).index(r)
+
+    def to_group(n, e, group, mask):
+        return copy(raw(n, e, col(0)), [(d, raw(n, e, col(slot_of(d, rank)))) for d in group], mask, "%s%s%d" % (n, e, rank))
+
+    def to_peers(n, e, first, w, sem="sent"):
+        call([copy(raw(n, e, col(first, NC, w)), [(p, raw(n, e, col(slot_of(p, me[first]), NC, w)))], split[j],
+                   "%s%s%d" % (n, e, me[first])) for j, p in enumerate(pe)], 2 * n_split, sem)
+
+    g.wait_ge(S.qx, 1)
+    for e in "qs":
+        call([to_group("x", e, [tw] if OPT["x"] == "fwd" else away, far)], n_far)
+    if OPT["x"] != "fwd":
+        for e in "qs":
+            to_peers("x", e, 0, 1, "sentm")
+    g.wait_ge(S.qw2, 1)
+    for e in "qs":
+        call([copy(raw("w2", e, slice(0, 256)), [(p, raw("wp", e, col(peers(p).index(rank), 256)))], split[j],
+                   "w%s%d" % (e, rank)) for j, p in enumerate(pe)], 2 * n_split)
+    if OPT["x"] == "fwd":
+        for e in "qs":
+            g.wait_ge(S["x%s%d" % (e, tw)], n_far)
+            to_peers("x", e, 0, 2, "sentm")
+    for n, off, sem in (("v", 1, "sentv"), ("u", 0, "sent")):
+        for j in range(2):
+            g.wait_ge(S["qt%d" % (2 + 2 * j + off)], 1)
+        for e in "qs":
+            call([copy(raw("t", e, col(2 + 2 * j + off)), [(p, raw("u", e, col(2 * peers(p).index(rank) + off)))], split[j],
+                       "%s%s%d" % (n, e, rank)) for j, p in enumerate(pe)], 2 * n_split, sem)
+    g.wait_ge(S.rb, 2)
+    call([copy(T.rb[:], [(tw, T.pc[:])], far, "pc")], n_far, "sentc")
+    g.wait_ge(S.qh, 1)
+    for e in "qs":
+        call([to_group("h", e, [tw] if OPT["h"] == "fwd" else away, far), to_group("h", e, pe, rest)], n_far + n_rest)
+    if OPT["h"] == "fwd":
+        for e in "qs":
+            g.wait_ge(S["h%s%d" % (e, tw)], n_far)
+            to_peers("h", e, 1, 1)
+
+    for n, b in (("x", "xb"), ("w1", "wb1"), ("w2", "wb2"), ("w3", "wb3")):
+        g.sync.dma_start(T[b][:], T[n][:]).then_inc(S["ld" + n], 16)
+    for s, gate in ((0, "sentm"), (1, None), (3, "sentv"), (5, None), (2, "sentc"), (4, None)):
+        if gate:
+            g.sync.wait_ge(S[gate], sent[gate])
+        g.sync.wait_ge(S["tA%d" % s], 2)
+        g.sync.wait_ge(S["tV%d" % s], 2)
+        g.sync.dma_start(T.t[me[s]], T.tt[:, col(s, 4 * NC)]).then_inc(S.stored, 16)
+    g.sync.wait_ge(S.hA, 3)
+    g.sync.wait_ge(S.hV, 1)
+    g.sync.dma_start(T.h[:], T.ht[:]).then_inc(S.stored, 16)
+    yorder = (0, 2, 4, 1, 3, 5)
+    for s in yorder:
+        g.sync.wait_ge(S["yc%d" % s], 2)
+        g.sync.dma_start(T.y[:, col(me[s], 256)], T.yb[:, col(s, 256)]).then_inc(S.stored, 16)
+    g.sync.wait_ge(S.stored, 16 * (2 * N + 1))
+    g.wait_ge(S.sent, sent["sent"])
+
+    relu, ident, add = ActivationFunctionType.Relu, ActivationFunctionType.Copy, AluOpType.add
+
+    def plus(out, src, c):
+        return g.vector.tensor_scalar(out, src, 0.0, c, AluOpType.max, AluOpType.mult)
+
+    def minus(out, src, c):
+        return g.vector.tensor_scalar(out, src, -c, 0.0, AluOpType.mult, AluOpType.max)
+
+    def row(buf, s, b):
+        return buf[:, 4 * NC * s + b:4 * NC * (s + 1):4]
+
+    def packed_view(name, sl):
+        return T[name + "q"][:, sl], T[name + "s"][:, sl]
+
+    def mm(b, w, wsl, x, xsl, start=True, stop=True):
+        wq, wsc = packed_view(w, wsl)
+        xq, xsc = packed_view(x, xsl)
+        return g.tensor.matmul_mx(bank(b), wq, wsc, xq, xsc, start, stop)
+
+    def landed(n, s, own_sem):
+        r = me[s]
+        if s == 0:
+            g.tensor.wait_ge(S[own_sem], 1)
+            return
+        if n == "h":
+            cnt = n_far if s == 1 or (s % 2 and OPT["h"] != "fwd") else (n_split if s % 2 else n_rest)
+        else:
+            if s > 1 and s % 2 and OPT["x"] == "fwd":
+                r = me[s - 1]
+            cnt = n_far if s == 1 or (s % 2 and OPT["x"] != "fwd") else n_split
+        for e in "qs":
+            g.tensor.wait_ge(S["%s%s%d" % (n, e, r)], cnt)
+
+    torder = (0, 1, 3, 5, 2, 4)
+    for k, s in enumerate(torder):
+        if s == 0:
+            g.tensor.wait_ge(S.qw1, 1)
+        if k >= 2:
+            g.tensor.wait_ge(S["tA%d" % torder[k - 2]], 2)
+            g.tensor.wait_ge(S["tV%d" % torder[k - 2]], 2)
+        landed("x", s, "qx")
+        for i, n in ((0, "za"), (1, "zb")):
+            mm(2 * (k % 2) + i, "w1", col(i), "x", col(s)).then_inc(S["%s%d" % (n, s)], 1)
+        if s < 2:
+            if s == 0:
+                g.tensor.wait_ge(S.qw2, 1)
+            g.tensor.wait_ge(S["qt%d" % s], 1)
+            for i in range(2):
+                mm(4 + 2 * s + i, "w2", col(i), "t", col(s), True, False)
+    for j, p in enumerate(pe):
+        for e in "qs":
+            g.tensor.wait_ge(S["w%s%d" % (e, p)], n_split)
+    for n, off, sem in (("v", 1, "sT"), ("u", 0, "own")):
+        for j, p in enumerate(pe):
+            for e in "qs":
+                g.tensor.wait_ge(S["%s%s%d" % (n, e, p)], n_split)
+            for i in range(2):
+                op = mm(4 + 2 * off + i, "wp", col(2 * j + i), "u", col(2 * j + off), False, j == 1)
+                if j == 1:
+                    op.then_inc(S[sem], 1)
+
+    for n, b in (("x", "xb"), ("w1", "wb1"), ("w2", "wb2")):
+        g.vector.wait_ge(S["ld" + n], 16)
+        oq, os = packed_view(n, slice(0, NC if n == "x" else 256))
+        g.vector.quantize_mx(oq, os, T[b][:]).then_inc(S["q" + n], 1)
+    for k, s in enumerate(torder):
+        b = 2 * (k % 2)
+        g.scalar.wait_ge(S["za%d" % s], 1)
+        g.scalar.activation(row(T.tt, s, 0), bank(b), relu, scale=C1).then_inc(S["tA%d" % s], 1)
+        g.scalar.activation(row(T.tt, s, 1), bank(b), relu, scale=-C1).then_inc(S["tA%d" % s], 1)
+        g.vector.wait_ge(S["zb%d" % s], 1)
+        plus(row(T.tt, s, 2), bank(b + 1), C1).then_inc(S["tV%d" % s], 1)
+        minus(row(T.tt, s, 3), bank(b + 1), C1).then_inc(S["tV%d" % s], 1)
+        g.vector.wait_ge(S["tV%d" % s], 2)
+        g.vector.wait_ge(S["tA%d" % s], 2)
+        oq, os = packed_view("t", col(s))
+        g.vector.quantize_mx(oq, os, T.tt[:, col(s, 4 * NC)]).then_inc(S["qt%d" % s], 1)
+        if s == 0:
+            g.vector.wait_ge(S.ldw3, 16)
+            oq, os = packed_view("w3", slice(0, 256))
+            g.vector.quantize_mx(oq, os, T.wb3[:]).then_inc(S.qw3, 1)
+
+    g.scalar.wait_ge(S.sT, 2)
+    g.scalar.activation(T.rb[:, col(0)], bank(6), ident).then_inc(S.rb, 1)
+    g.vector.wait_ge(S.sT, 2)
+    g.vector.tensor_copy(T.rb[:, col(1)], bank(7)).then_inc(S.rb, 1)
+
+    g.vector.wait_ge(S.own, 2)
+    g.vector.wait_ge(S.pc, n_far)
+    for i in range(2):
+        g.vector.tensor_tensor(T.sf[:, col(i)], bank(4 + i), T.pc[:, col(i)], add).then_inc(S["sf%d" % i], 1)
+    g.scalar.wait_ge(S.sf0, 1)
+    g.scalar.activation(row(T.ht, 0, 0), T.sf[:, col(0)], relu, scale=C2).then_inc(S.hA, 1)
+    g.scalar.activation(row(T.ht, 0, 1), T.sf[:, col(0)], relu, scale=-C2).then_inc(S.hA, 1)
+    g.scalar.wait_ge(S.sf1, 1)
+    g.scalar.activation(row(T.ht, 0, 2), T.sf[:, col(1)], relu, scale=C2).then_inc(S.hA, 1)
+    g.vector.wait_ge(S.sf1, 1)
+    minus(row(T.ht, 0, 3), T.sf[:, col(1)], C2).then_inc(S.hV, 1)
+    g.vector.wait_ge(S.hV, 1)
+    g.vector.wait_ge(S.hA, 3)
+    oq, os = packed_view("h", col(0))
+    g.vector.quantize_mx(oq, os, T.ht[:]).then_inc(S.qh, 1)
+
+    g.tensor.wait_ge(S.qw3, 1)
+    g.tensor.wait_ge(S.rb, 2)
+    for s in torder[4:]:
+        g.tensor.wait_ge(S["tA%d" % s], 2)
+        g.tensor.wait_ge(S["tV%d" % s], 2)
+    pairs = (0, 2, 6)
+    for k, s in enumerate(yorder):
+        b = pairs[k % 3]
+        if k >= 3:
+            g.tensor.wait_ge(S["yc%d" % yorder[k - 3]], 2)
+        landed("h", s, "qh")
+        for i, n in ((0, "ya"), (1, "yv")):
+            mm(b + i, "w3", col(i), "h", col(s)).then_inc(S["%s%d" % (n, s)], 1)
+        g.scalar.wait_ge(S["ya%d" % s], 1)
+        g.scalar.activation(T.yb[:, col(2 * s)], bank(b), ident).then_inc(S["yc%d" % s], 1)
+        g.vector.wait_ge(S["yv%d" % s], 1)
+        g.vector.tensor_copy(T.yb[:, col(2 * s + 1)], bank(b + 1)).then_inc(S["yc%d" % s], 1)

@@ -7,7 +7,7 @@ NC = 128
 C1 = float(np.float32(0.043))
 C2 = float(np.float32(0.01755))
 CODES = "float8_e4m3fn_x4"
-OPT = {"x": "fwd", "h": "fwd"}
+VIA_TWIN = "h"
 
 
 def packed(name, n):
@@ -36,10 +36,14 @@ SCRATCH.update(packed("t", N * NC))
 SCRATCH.update(packed("u", 4 * NC))
 SCRATCH.update(packed("h", N * NC))
 
-SEMAPHORES = (["ldx", "ldw1", "ldw2", "ldw3", "qx", "qw1", "qw2", "qw3", "sent", "sentm", "sentv", "sentc", "stored",
-               "own", "rb", "pc", "sf0", "sf1", "sT", "hA", "hV", "qh"]
+SEMAPHORES = (["ldx", "ldw1", "ldw2", "ldw3", "qx", "qw1", "qw2", "qw3", "sent", "sentv", "sentc", "stored", "tR",
+               "own0", "own1", "rb0", "rb1", "sT0", "sT1", "pc0", "pc1", "sf0", "sf1", "hA", "hV", "qh"]
               + ["%s%s%d" % (n, e, r) for n in "xhwuv" for e in "qs" for r in range(N)]
               + ["%s%d" % (n, s) for n in ("za", "zb", "tA", "tV", "qt", "ya", "yv", "yc") for s in range(N)])
+
+TILES = (0, 1, 3, 5, 2, 4)
+SHARED = 5
+OUTS = (0, 1, 2, 4, 3, 5)
 
 
 def rank_program(g, core, T, topo):
@@ -67,6 +71,9 @@ def rank_program(g, core, T, topo):
             out += [q, twin(q)]
         return out
 
+    def slot_of(d, r):
+        return slots(d).index(r)
+
     def dst(r):
         rid, pid, _ = topo.addr(cores[r])
         return DstId(rid=rid, pnc=pid)
@@ -75,17 +82,17 @@ def rank_program(g, core, T, topo):
         return [e for e in range(16) if (m >> e) & 1]
 
     me, pe, tw = slots(rank), peers(rank), twin(rank)
-    away = [r for r in range(N) if r not in home(rank)]
+    away = [tw] + [r for r in range(N) if r not in home(rank) and r != tw]
     far = topo.mask(core, cores[tw])
     near = topo.mask(core, cores[pe[0]])
     rest = near & ~far
     nb = bits(near)
     split = [sum(1 << e for e in nb[0::2]), sum(1 << e for e in nb[1::2])]
-    n_far, n_rest, n_split = len(bits(far)), len(bits(rest)), len(bits(split[0]))
+    n_far, n_rest, n_split, n_near = len(bits(far)), len(bits(rest)), len(bits(split[0])), len(nb)
     sent = {}
 
-    def col(s, w=NC, n=1):
-        return slice(w * s, w * (s + n))
+    def col(s, w=NC):
+        return slice(w * s, w * (s + 1))
 
     def raw(name, e, sl):
         v = T[name + e][:, sl]
@@ -102,63 +109,70 @@ def rank_program(g, core, T, topo):
         g.remote_dma_fused(transfers, local_sem=S[sem])
         sent[sem] = sent.get(sem, 0) + n
 
-    def slot_of(d, r):
-        return slots(d).index(r)
-
     def to_group(n, e, group, mask):
         return copy(raw(n, e, col(0)), [(d, raw(n, e, col(slot_of(d, rank)))) for d in group], mask, "%s%s%d" % (n, e, rank))
 
-    def to_peers(n, e, first, w, sem="sent"):
-        call([copy(raw(n, e, col(first, NC, w)), [(p, raw(n, e, col(slot_of(p, me[first]), NC, w)))], split[j],
-                   "%s%s%d" % (n, e, me[first])) for j, p in enumerate(pe)], 2 * n_split, sem)
+    def cross(n):
+        return [tw] if n in VIA_TWIN else away
+
+    def pass_on(n):
+        for e in ("qs" if n in VIA_TWIN else "q"):
+            g.wait_ge(S["%s%s%d" % (n, e, tw)], n_far)
+            call([copy(raw(n, e, col(1)), [(p, raw(n, e, col(slot_of(p, tw))))], split[j], "%s%s%d" % (n, e, tw))
+                  for j, p in enumerate(pe)], 2 * n_split)
+
+    def t_to(j, e, off, mask, n):
+        p = pe[j]
+        return copy(raw("t", e, col(2 + 2 * j + off)), [(p, raw("u", e, col(2 * peers(p).index(rank) + off)))], mask,
+                    "%s%s%d" % (n, e, rank))
 
     g.wait_ge(S.qx, 1)
-    for e in "qs":
-        call([to_group("x", e, [tw] if OPT["x"] == "fwd" else away, far)], n_far)
-    if OPT["x"] != "fwd":
-        for e in "qs":
-            to_peers("x", e, 0, 1, "sentm")
+    call([to_group("x", "q", [tw], far)], n_far)
+    call([to_group("x", "s", cross("x"), far), to_group("x", "s", pe, rest)], n_far + n_rest)
+    call([to_group("x", "q", pe, rest)], n_rest)
+    pass_on("x")
     g.wait_ge(S.qw2, 1)
     for e in "qs":
-        call([copy(raw("w2", e, slice(0, 256)), [(p, raw("wp", e, col(peers(p).index(rank), 256)))], split[j],
+        call([copy(raw("w2", e, col(0, 256)), [(p, raw("wp", e, col(peers(p).index(rank), 256)))], split[j],
                    "w%s%d" % (e, rank)) for j, p in enumerate(pe)], 2 * n_split)
-    if OPT["x"] == "fwd":
+    for j in range(2):
+        g.wait_ge(S["qt%d" % (3 + 2 * j)], 1)
         for e in "qs":
-            g.wait_ge(S["x%s%d" % (e, tw)], n_far)
-            to_peers("x", e, 0, 2, "sentm")
-    for n, off, sem in (("v", 1, "sentv"), ("u", 0, "sent")):
-        for j in range(2):
-            g.wait_ge(S["qt%d" % (2 + 2 * j + off)], 1)
-        for e in "qs":
-            call([copy(raw("t", e, col(2 + 2 * j + off)), [(p, raw("u", e, col(2 * peers(p).index(rank) + off)))], split[j],
-                       "%s%s%d" % (n, e, rank)) for j, p in enumerate(pe)], 2 * n_split, sem)
-    g.wait_ge(S.rb, 2)
-    call([copy(T.rb[:], [(tw, T.pc[:])], far, "pc")], n_far, "sentc")
-    g.wait_ge(S.qh, 1)
+            call([t_to(j, e, 1, near, "v")], n_near, "sentv")
+    for j in range(2):
+        g.wait_ge(S["qt%d" % (2 + 2 * j)], 1)
     for e in "qs":
-        call([to_group("h", e, [tw] if OPT["h"] == "fwd" else away, far), to_group("h", e, pe, rest)], n_far + n_rest)
-    if OPT["h"] == "fwd":
-        for e in "qs":
-            g.wait_ge(S["h%s%d" % (e, tw)], n_far)
-            to_peers("h", e, 1, 1)
+        call([t_to(j, e, 0, split[j], "u") for j in range(2)], 2 * n_split)
+    for i in range(2):
+        g.wait_ge(S["rb%d" % i], 1)
+        call([copy(T.rb[:, col(i)], [(tw, T.pc[:, col(i)])], far, "pc%d" % i)], n_far, "sentc")
+    g.wait_ge(S.qh, 1)
+    call([to_group("h", "q", [tw], far), to_group("h", "q", pe, rest)], n_far + n_rest)
+    call([to_group("h", "s", cross("h"), far), to_group("h", "s", pe, rest)], n_far + n_rest)
+    pass_on("h")
 
     for n, b in (("x", "xb"), ("w1", "wb1"), ("w2", "wb2"), ("w3", "wb3")):
         g.sync.dma_start(T[b][:], T[n][:]).then_inc(S["ld" + n], 16)
-    for s, gate in ((0, "sentm"), (1, None), (3, "sentv"), (5, None), (2, "sentc"), (4, None)):
+
+    def tile_done(queue, s):
+        queue.wait_ge(S["tA%d" % s], 2)
+        queue.wait_ge(S["tV%d" % s], 1 if s == SHARED else 2)
+
+    for s, gate in ((1, None), (0, None), (3, "sentv"), (5, None), (2, "sentc"), (4, None)):
         if gate:
             g.sync.wait_ge(S[gate], sent[gate])
-        g.sync.wait_ge(S["tA%d" % s], 2)
-        g.sync.wait_ge(S["tV%d" % s], 2)
+        tile_done(g.sync, s)
         g.sync.dma_start(T.t[me[s]], T.tt[:, col(s, 4 * NC)]).then_inc(S.stored, 16)
-    g.sync.wait_ge(S.hA, 3)
-    g.sync.wait_ge(S.hV, 1)
-    g.sync.dma_start(T.h[:], T.ht[:]).then_inc(S.stored, 16)
-    yorder = (0, 2, 4, 1, 3, 5)
-    for s in yorder:
+    for s in OUTS:
         g.sync.wait_ge(S["yc%d" % s], 2)
         g.sync.dma_start(T.y[:, col(me[s], 256)], T.yb[:, col(s, 256)]).then_inc(S.stored, 16)
+        if s == 0:
+            g.sync.wait_ge(S.hA, 3)
+            g.sync.wait_ge(S.hV, 1)
+            g.sync.dma_start(T.h[:], T.ht[:]).then_inc(S.stored, 16)
     g.sync.wait_ge(S.stored, 16 * (2 * N + 1))
-    g.wait_ge(S.sent, sent["sent"])
+    for k in ("sent", "sentv", "sentc"):
+        g.wait_ge(S[k], sent[k])
 
     relu, ident, add = ActivationFunctionType.Relu, ActivationFunctionType.Copy, AluOpType.add
 
@@ -171,85 +185,86 @@ def rank_program(g, core, T, topo):
     def row(buf, s, b):
         return buf[:, 4 * NC * s + b:4 * NC * (s + 1):4]
 
-    def packed_view(name, sl):
+    def pair(name, sl):
         return T[name + "q"][:, sl], T[name + "s"][:, sl]
 
     def mm(b, w, wsl, x, xsl, start=True, stop=True):
-        wq, wsc = packed_view(w, wsl)
-        xq, xsc = packed_view(x, xsl)
+        wq, wsc = pair(w, wsl)
+        xq, xsc = pair(x, xsl)
         return g.tensor.matmul_mx(bank(b), wq, wsc, xq, xsc, start, stop)
 
-    def landed(n, s, own_sem):
-        r = me[s]
-        if s == 0:
-            g.tensor.wait_ge(S[own_sem], 1)
-            return
-        if n == "h":
-            cnt = n_far if s == 1 or (s % 2 and OPT["h"] != "fwd") else (n_split if s % 2 else n_rest)
-        else:
-            if s > 1 and s % 2 and OPT["x"] == "fwd":
-                r = me[s - 1]
-            cnt = n_far if s == 1 or (s % 2 and OPT["x"] != "fwd") else n_split
-        for e in "qs":
-            g.tensor.wait_ge(S["%s%s%d" % (n, e, r)], cnt)
+    def quantise(name, sl, tile, sem):
+        q, sc = pair(name, sl)
+        g.vector.quantize_mx(q, sc, tile).then_inc(S[sem], 1)
 
-    torder = (0, 1, 3, 5, 2, 4)
-    for k, s in enumerate(torder):
+    def landed(n, s, own):
+        if s == 0:
+            g.tensor.wait_ge(S[own], 1)
+            return
+        if s % 2:
+            nq = n_far if s == 1 else n_split
+            ns = n_split if s > 1 and n in VIA_TWIN else n_far
+        else:
+            nq = ns = n_rest
+        g.tensor.wait_ge(S["%sq%d" % (n, me[s])], nq)
+        g.tensor.wait_ge(S["%ss%d" % (n, me[s])], ns)
+
+    for k, s in enumerate(TILES):
         if s == 0:
             g.tensor.wait_ge(S.qw1, 1)
         if k >= 2:
-            g.tensor.wait_ge(S["tA%d" % torder[k - 2]], 2)
-            g.tensor.wait_ge(S["tV%d" % torder[k - 2]], 2)
+            tile_done(g.tensor, TILES[k - 2])
         landed("x", s, "qx")
-        for i, n in ((0, "za"), (1, "zb")):
-            mm(2 * (k % 2) + i, "w1", col(i), "x", col(s)).then_inc(S["%s%d" % (n, s)], 1)
+        for i in ((1, 0) if s == SHARED else (0, 1)):
+            mm(2 * (k % 2) + i, "w1", col(i), "x", col(s)).then_inc(S["%s%d" % (("za", "zb")[i], s)], 1)
         if s < 2:
             if s == 0:
                 g.tensor.wait_ge(S.qw2, 1)
             g.tensor.wait_ge(S["qt%d" % s], 1)
             for i in range(2):
                 mm(4 + 2 * s + i, "w2", col(i), "t", col(s), True, False)
-    for j, p in enumerate(pe):
+    for p in pe:
         for e in "qs":
             g.tensor.wait_ge(S["w%s%d" % (e, p)], n_split)
-    for n, off, sem in (("v", 1, "sT"), ("u", 0, "own")):
-        for j, p in enumerate(pe):
+    for n, off, sem, cnt in (("v", 1, "sT", n_near), ("u", 0, "own", n_split)):
+        for j in (1, 0):
             for e in "qs":
-                g.tensor.wait_ge(S["%s%s%d" % (n, e, p)], n_split)
+                g.tensor.wait_ge(S["%s%s%d" % (n, e, pe[j])], cnt)
             for i in range(2):
-                op = mm(4 + 2 * off + i, "wp", col(2 * j + i), "u", col(2 * j + off), False, j == 1)
-                if j == 1:
-                    op.then_inc(S[sem], 1)
+                op = mm(4 + 2 * off + i, "wp", col(2 * j + i), "u", col(2 * j + off), False, j == 0)
+                if j == 0:
+                    op.then_inc(S["%s%d" % (sem, i)], 1)
 
     for n, b in (("x", "xb"), ("w1", "wb1"), ("w2", "wb2")):
         g.vector.wait_ge(S["ld" + n], 16)
-        oq, os = packed_view(n, slice(0, NC if n == "x" else 256))
-        g.vector.quantize_mx(oq, os, T[b][:]).then_inc(S["q" + n], 1)
-    for k, s in enumerate(torder):
+        quantise(n, slice(0, NC if n == "x" else 256), T[b][:], "q" + n)
+    for k, s in enumerate(TILES):
         b = 2 * (k % 2)
+        g.vector.wait_ge(S["zb%d" % s], 1)
+        if s == SHARED:
+            g.scalar.wait_ge(S["zb%d" % s], 1)
+            g.scalar.activation(row(T.tt, s, 2), bank(b + 1), relu, scale=C1).then_inc(S.tR, 1)
+            g.vector.wait_ge(S.tR, 1)
+        else:
+            plus(row(T.tt, s, 2), bank(b + 1), C1).then_inc(S["tV%d" % s], 1)
+        minus(row(T.tt, s, 3), bank(b + 1), C1).then_inc(S["tV%d" % s], 1)
         g.scalar.wait_ge(S["za%d" % s], 1)
         g.scalar.activation(row(T.tt, s, 0), bank(b), relu, scale=C1).then_inc(S["tA%d" % s], 1)
         g.scalar.activation(row(T.tt, s, 1), bank(b), relu, scale=-C1).then_inc(S["tA%d" % s], 1)
-        g.vector.wait_ge(S["zb%d" % s], 1)
-        plus(row(T.tt, s, 2), bank(b + 1), C1).then_inc(S["tV%d" % s], 1)
-        minus(row(T.tt, s, 3), bank(b + 1), C1).then_inc(S["tV%d" % s], 1)
-        g.vector.wait_ge(S["tV%d" % s], 2)
-        g.vector.wait_ge(S["tA%d" % s], 2)
-        oq, os = packed_view("t", col(s))
-        g.vector.quantize_mx(oq, os, T.tt[:, col(s, 4 * NC)]).then_inc(S["qt%d" % s], 1)
+        tile_done(g.vector, s)
+        quantise("t", col(s), T.tt[:, col(s, 4 * NC)], "qt%d" % s)
         if s == 0:
             g.vector.wait_ge(S.ldw3, 16)
-            oq, os = packed_view("w3", slice(0, 256))
-            g.vector.quantize_mx(oq, os, T.wb3[:]).then_inc(S.qw3, 1)
+            quantise("w3", slice(0, 256), T.wb3[:], "qw3")
 
-    g.scalar.wait_ge(S.sT, 2)
-    g.scalar.activation(T.rb[:, col(0)], bank(6), ident).then_inc(S.rb, 1)
-    g.vector.wait_ge(S.sT, 2)
-    g.vector.tensor_copy(T.rb[:, col(1)], bank(7)).then_inc(S.rb, 1)
+    g.scalar.wait_ge(S.sT0, 1)
+    g.scalar.activation(T.rb[:, col(0)], bank(6), ident).then_inc(S.rb0, 1)
+    g.vector.wait_ge(S.sT1, 1)
+    g.vector.tensor_copy(T.rb[:, col(1)], bank(7)).then_inc(S.rb1, 1)
 
-    g.vector.wait_ge(S.own, 2)
-    g.vector.wait_ge(S.pc, n_far)
     for i in range(2):
+        g.vector.wait_ge(S["own%d" % i], 1)
+        g.vector.wait_ge(S["pc%d" % i], n_far)
         g.vector.tensor_tensor(T.sf[:, col(i)], bank(4 + i), T.pc[:, col(i)], add).then_inc(S["sf%d" % i], 1)
     g.scalar.wait_ge(S.sf0, 1)
     g.scalar.activation(row(T.ht, 0, 0), T.sf[:, col(0)], relu, scale=C2).then_inc(S.hA, 1)
@@ -260,19 +275,17 @@ def rank_program(g, core, T, topo):
     minus(row(T.ht, 0, 3), T.sf[:, col(1)], C2).then_inc(S.hV, 1)
     g.vector.wait_ge(S.hV, 1)
     g.vector.wait_ge(S.hA, 3)
-    oq, os = packed_view("h", col(0))
-    g.vector.quantize_mx(oq, os, T.ht[:]).then_inc(S.qh, 1)
+    quantise("h", col(0), T.ht[:], "qh")
 
     g.tensor.wait_ge(S.qw3, 1)
-    g.tensor.wait_ge(S.rb, 2)
-    for s in torder[4:]:
-        g.tensor.wait_ge(S["tA%d" % s], 2)
-        g.tensor.wait_ge(S["tV%d" % s], 2)
-    pairs = (0, 2, 6)
-    for k, s in enumerate(yorder):
-        b = pairs[k % 3]
+    g.tensor.wait_ge(S.rb0, 1)
+    g.tensor.wait_ge(S.rb1, 1)
+    for s in TILES[4:]:
+        tile_done(g.tensor, s)
+    for k, s in enumerate(OUTS):
+        b = (0, 2, 6)[k % 3]
         if k >= 3:
-            g.tensor.wait_ge(S["yc%d" % yorder[k - 3]], 2)
+            g.tensor.wait_ge(S["yc%d" % OUTS[k - 3]], 2)
         landed("h", s, "qh")
         for i, n in ((0, "ya"), (1, "yv")):
             mm(b + i, "w3", col(i), "h", col(s)).then_inc(S["%s%d" % (n, s)], 1)

@@ -7,7 +7,6 @@ NC = 128
 C1 = float(np.float32(0.043))
 C2 = float(np.float32(0.01755))
 CODES = "float8_e4m3fn_x4"
-VIA_TWIN = "h"
 
 
 def packed(name, n):
@@ -20,10 +19,10 @@ SCRATCH = {
     "wb2": ("sbuf", [128, 1024], "bfloat16"),
     "wb3": ("sbuf", [128, 1024], "bfloat16"),
     "tt": ("sbuf", [128, N * 4 * NC], "bfloat16"),
-    "ht": ("sbuf", [128, 4 * NC], "bfloat16"),
-    "rb": ("sbuf", [128, 256], "float32"),
-    "pc": ("sbuf", [128, 256], "float32"),
-    "sf": ("sbuf", [128, 256], "float32"),
+    "ht": ("sbuf", [128, 2 * 4 * NC], "bfloat16"),
+    "ra": ("sbuf", [128, 512], "float32"),
+    "pc": ("sbuf", [128, 512], "float32"),
+    "sf": ("sbuf", [128, 512], "float32"),
     "yb": ("sbuf", [128, N * 256], "float32"),
     "ps": ("psum", [128, 512 * 8], "float32"),
 }
@@ -36,14 +35,17 @@ SCRATCH.update(packed("t", N * NC))
 SCRATCH.update(packed("u", 4 * NC))
 SCRATCH.update(packed("h", N * NC))
 
-SEMAPHORES = (["ldx", "ldw1", "ldw2", "ldw3", "qx", "qw1", "qw2", "qw3", "sent", "sentv", "sentc", "stored", "tR",
-               "own0", "own1", "rb0", "rb1", "sT0", "sT1", "pc0", "pc1", "sf0", "sf1", "hA", "hV", "qh"]
+LEFT = "xpwuvecgh"
+SEMAPHORES = (["ldx", "ldw1", "ldw2", "ldw3", "qx", "qw1", "qw2", "qw3", "stored"]
+              + ["left" + n for n in LEFT]
+              + ["%s%d" % (n, i) for n in ("sum", "out", "sf") for i in range(4)]
+              + ["%s%d" % (n, k) for n in ("pc", "hA", "hV", "qh") for k in range(2)]
               + ["%s%s%d" % (n, e, r) for n in "xhwuv" for e in "qs" for r in range(N)]
               + ["%s%d" % (n, s) for n in ("za", "zb", "tA", "tV", "qt", "ya", "yv", "yc") for s in range(N)])
 
-TILES = (0, 1, 3, 5, 2, 4)
-SHARED = 5
-OUTS = (0, 1, 2, 4, 3, 5)
+GROUPS = ((0,), (4, 2), (1,), (3, 5))
+OUTS = (1, 0, 3, 5, 4, 2)
+STORES = "t4 >p t0 >e t2 t5 t1 >c t3 h y0 y135 >h y4 y2".split()
 
 
 def rank_program(g, core, T, topo):
@@ -88,7 +90,7 @@ def rank_program(g, core, T, topo):
     rest = near & ~far
     nb = bits(near)
     split = [sum(1 << e for e in nb[0::2]), sum(1 << e for e in nb[1::2])]
-    n_far, n_rest, n_split, n_near = len(bits(far)), len(bits(rest)), len(bits(split[0])), len(nb)
+    n_far, n_rest, n_split = len(bits(far)), len(bits(rest)), len(bits(split[0]))
     sent = {}
 
     def col(s, w=NC):
@@ -105,74 +107,82 @@ def rank_program(g, core, T, topo):
         return RemoteDMATransfer(dst_ids=[dst(d) for d, _ in dsts], dma_engine_mask=mask, remote_sem=S[sem],
                                  srcs=[src], dsts=[a for _, a in dsts], alu_op=0)
 
-    def call(transfers, n, sem="sent"):
-        g.remote_dma_fused(transfers, local_sem=S[sem])
-        sent[sem] = sent.get(sem, 0) + n
+    def call(transfers, n, what):
+        g.remote_dma_fused(transfers, local_sem=S["left" + what])
+        sent[what] = sent.get(what, 0) + n
+
+    def gone(queue, what):
+        queue.wait_ge(S["left" + what], sent[what])
 
     def to_group(n, e, group, mask):
         return copy(raw(n, e, col(0)), [(d, raw(n, e, col(slot_of(d, rank)))) for d in group], mask, "%s%s%d" % (n, e, rank))
 
-    def cross(n):
-        return [tw] if n in VIA_TWIN else away
+    def to_peers(n, e, s, what):
+        r = me[s]
+        call([copy(raw(n, e, col(s)), [(p, raw(n, e, col(slot_of(p, r))))], split[j], "%s%s%d" % (n, e, r))
+              for j, p in enumerate(pe)], 2 * n_split, what)
 
-    def pass_on(n):
-        for e in ("qs" if n in VIA_TWIN else "q"):
-            g.wait_ge(S["%s%s%d" % (n, e, tw)], n_far)
-            call([copy(raw(n, e, col(1)), [(p, raw(n, e, col(slot_of(p, tw))))], split[j], "%s%s%d" % (n, e, tw))
-                  for j, p in enumerate(pe)], 2 * n_split)
+    def t_to_peers(off, what):
+        for j in range(2):
+            g.wait_ge(S["qt%d" % (2 + 2 * j + off)], 1)
+        for e in "qs":
+            call([copy(raw("t", e, col(2 + 2 * j + off)), [(p, raw("u", e, col(2 * peers(p).index(rank) + off)))],
+                       split[j], "%s%s%d" % (what, e, rank)) for j, p in enumerate(pe)], 2 * n_split, what)
 
-    def t_to(j, e, off, mask, n):
-        p = pe[j]
-        return copy(raw("t", e, col(2 + 2 * j + off)), [(p, raw("u", e, col(2 * peers(p).index(rank) + off)))], mask,
-                    "%s%s%d" % (n, e, rank))
+    def sum_out(k, what):
+        for i in range(2):
+            g.wait_ge(S["out%d" % (2 * k + i)], 1)
+        call([copy(T.ra[:, col(k, 256)], [(tw, T.pc[:, col(1 - k, 256)])], far, "pc%d" % (1 - k))], n_far, what)
 
     g.wait_ge(S.qx, 1)
-    call([to_group("x", "q", [tw], far)], n_far)
-    call([to_group("x", "s", cross("x"), far), to_group("x", "s", pe, rest)], n_far + n_rest)
-    call([to_group("x", "q", pe, rest)], n_rest)
-    pass_on("x")
+    call([to_group("x", "q", [tw], far), to_group("x", "q", pe, rest)], n_far + n_rest, "x")
+    call([to_group("x", "s", away, far), to_group("x", "s", pe, rest)], n_far + n_rest, "x")
+    g.wait_ge(S["xq%d" % tw], n_far)
+    to_peers("x", "q", 1, "p")
     g.wait_ge(S.qw2, 1)
     for e in "qs":
         call([copy(raw("w2", e, col(0, 256)), [(p, raw("wp", e, col(peers(p).index(rank), 256)))], split[j],
-                   "w%s%d" % (e, rank)) for j, p in enumerate(pe)], 2 * n_split)
-    for j in range(2):
-        g.wait_ge(S["qt%d" % (3 + 2 * j)], 1)
+                   "w%s%d" % (e, rank)) for j, p in enumerate(pe)], 2 * n_split, "w")
+    t_to_peers(0, "u")
+    t_to_peers(1, "v")
+    sum_out(0, "e")
+    sum_out(1, "c")
+    for k, what in ((1, "g"), (0, "h")):
+        g.wait_ge(S["qh%d" % k], 1)
         for e in "qs":
-            call([t_to(j, e, 1, near, "v")], n_near, "sentv")
-    for j in range(2):
-        g.wait_ge(S["qt%d" % (2 + 2 * j)], 1)
-    for e in "qs":
-        call([t_to(j, e, 0, split[j], "u") for j in range(2)], 2 * n_split)
-    for i in range(2):
-        g.wait_ge(S["rb%d" % i], 1)
-        call([copy(T.rb[:, col(i)], [(tw, T.pc[:, col(i)])], far, "pc%d" % i)], n_far, "sentc")
-    g.wait_ge(S.qh, 1)
-    call([to_group("h", "q", [tw], far), to_group("h", "q", pe, rest)], n_far + n_rest)
-    call([to_group("h", "s", cross("h"), far), to_group("h", "s", pe, rest)], n_far + n_rest)
-    pass_on("h")
+            to_peers("h", e, k, what)
 
     for n, b in (("x", "xb"), ("w1", "wb1"), ("w2", "wb2"), ("w3", "wb3")):
         g.sync.dma_start(T[b][:], T[n][:]).then_inc(S["ld" + n], 16)
 
     def tile_done(queue, s):
         queue.wait_ge(S["tA%d" % s], 2)
-        queue.wait_ge(S["tV%d" % s], 1 if s == SHARED else 2)
+        queue.wait_ge(S["tV%d" % s], 2)
 
-    for s, gate in ((1, None), (0, None), (3, "sentv"), (5, None), (2, "sentc"), (4, None)):
-        if gate:
-            g.sync.wait_ge(S[gate], sent[gate])
-        tile_done(g.sync, s)
-        g.sync.dma_start(T.t[me[s]], T.tt[:, col(s, 4 * NC)]).then_inc(S.stored, 16)
-    for s in OUTS:
-        g.sync.wait_ge(S["yc%d" % s], 2)
-        g.sync.dma_start(T.y[:, col(me[s], 256)], T.yb[:, col(s, 256)]).then_inc(S.stored, 16)
-        if s == 0:
-            g.sync.wait_ge(S.hA, 3)
-            g.sync.wait_ge(S.hV, 1)
-            g.sync.dma_start(T.h[:], T.ht[:]).then_inc(S.stored, 16)
-    g.sync.wait_ge(S.stored, 16 * (2 * N + 1))
-    for k in ("sent", "sentv", "sentc"):
-        g.wait_ge(S[k], sent[k])
+    def store(out, in_):
+        g.sync.dma_start(out, in_).then_inc(S.stored, 16)
+
+    for what in STORES:
+        if what[0] == ">":
+            gone(g.sync, what[1])
+        elif what[0] == "t":
+            s = int(what[1])
+            tile_done(g.sync, s)
+            store(T.t[me[s]], T.tt[:, col(s, 4 * NC)])
+        elif what[0] == "y":
+            ranks = []
+            for s in what[1:]:
+                g.sync.wait_ge(S["yc" + s], 2)
+                ranks.append(me[int(s)])
+            c = slice(256 * min(ranks), 256 * (max(ranks) + 1))
+            store(T.y[:, c], T.yb[:, c])
+        else:
+            g.sync.wait_ge(S.hA0, 3)
+            g.sync.wait_ge(S.hV0, 1)
+            store(T.h[:], T.ht[:, col(0, 4 * NC)])
+    g.sync.wait_ge(S.stored, 16 * len([w for w in STORES if w[0] != ">"]))
+    for k in LEFT:
+        gone(g, k)
 
     relu, ident, add = ActivationFunctionType.Relu, ActivationFunctionType.Copy, AluOpType.add
 
@@ -197,99 +207,106 @@ def rank_program(g, core, T, topo):
         q, sc = pair(name, sl)
         g.vector.quantize_mx(q, sc, tile).then_inc(S[sem], 1)
 
-    def landed(n, s, own):
-        if s == 0:
-            g.tensor.wait_ge(S[own], 1)
-            return
-        if s % 2:
-            nq = n_far if s == 1 else n_split
-            ns = n_split if s > 1 and n in VIA_TWIN else n_far
-        else:
-            nq = ns = n_rest
-        g.tensor.wait_ge(S["%sq%d" % (n, me[s])], nq)
-        g.tensor.wait_ge(S["%ss%d" % (n, me[s])], ns)
+    tiles = [s for group in GROUPS for s in group]
 
-    for k, s in enumerate(TILES):
+    def x_landed(s):
         if s == 0:
-            g.tensor.wait_ge(S.qw1, 1)
-        if k >= 2:
-            tile_done(g.tensor, TILES[k - 2])
-        landed("x", s, "qx")
-        for i in ((1, 0) if s == SHARED else (0, 1)):
-            mm(2 * (k % 2) + i, "w1", col(i), "x", col(s)).then_inc(S["%s%d" % (("za", "zb")[i], s)], 1)
-        if s < 2:
-            if s == 0:
-                g.tensor.wait_ge(S.qw2, 1)
-            g.tensor.wait_ge(S["qt%d" % s], 1)
-            for i in range(2):
-                mm(4 + 2 * s + i, "w2", col(i), "t", col(s), True, False)
-    for p in pe:
-        for e in "qs":
-            g.tensor.wait_ge(S["w%s%d" % (e, p)], n_split)
-    for n, off, sem, cnt in (("v", 1, "sT", n_near), ("u", 0, "own", n_split)):
+            g.tensor.wait_ge(S.qx, 1)
+            return
+        g.tensor.wait_ge(S["xq%d" % me[s]], n_rest if s % 2 == 0 else n_far if s == 1 else n_split)
+        g.tensor.wait_ge(S["xs%d" % me[s]], n_far if s % 2 else n_rest)
+
+    def own_term(k):
+        g.tensor.wait_ge(S.qw2, 1)
+        g.tensor.wait_ge(S["qt%d" % k], 1)
+        tile_done(g.tensor, tiles[2 + k])
+        for i in range(2):
+            mm(4 + 2 * k + i, "w2", col(i), "t", col(k), True, False)
+
+    g.tensor.wait_ge(S.qw1, 1)
+    for k, s in enumerate(tiles):
+        if k >= 4:
+            tile_done(g.tensor, tiles[k - 4])
+        x_landed(s)
+        for i in range(2):
+            mm(2 * (k % 4) + i, "w1", col(i), "x", col(s)).then_inc(S["%s%d" % (("za", "zb")[i], s)], 1)
+        if k == 3:
+            own_term(0)
+    for k, n in ((0, "u"), (1, "v")):
+        if k:
+            own_term(1)
         for j in (1, 0):
+            if k == 0:
+                for e in "qs":
+                    g.tensor.wait_ge(S["w%s%d" % (e, pe[j])], n_split)
             for e in "qs":
-                g.tensor.wait_ge(S["%s%s%d" % (n, e, pe[j])], cnt)
+                g.tensor.wait_ge(S["%s%s%d" % (n, e, pe[j])], n_split)
             for i in range(2):
-                op = mm(4 + 2 * off + i, "wp", col(2 * j + i), "u", col(2 * j + off), False, j == 0)
+                op = mm(4 + 2 * k + i, "wp", col(2 * j + i), "u", col(2 * j + k), False, j == 0)
                 if j == 0:
-                    op.then_inc(S["%s%d" % (sem, i)], 1)
+                    op.then_inc(S["sum%d" % (2 * k + i)], 1)
 
     for n, b in (("x", "xb"), ("w1", "wb1"), ("w2", "wb2")):
         g.vector.wait_ge(S["ld" + n], 16)
         quantise(n, slice(0, NC if n == "x" else 256), T[b][:], "q" + n)
-    for k, s in enumerate(TILES):
-        b = 2 * (k % 2)
-        g.vector.wait_ge(S["zb%d" % s], 1)
-        if s == SHARED:
-            g.scalar.wait_ge(S["zb%d" % s], 1)
-            g.scalar.activation(row(T.tt, s, 2), bank(b + 1), relu, scale=C1).then_inc(S.tR, 1)
-            g.vector.wait_ge(S.tR, 1)
-        else:
+    for group in GROUPS:
+        for s in group:
+            b = 2 * (tiles.index(s) % 4)
+            g.vector.wait_ge(S["zb%d" % s], 1)
             plus(row(T.tt, s, 2), bank(b + 1), C1).then_inc(S["tV%d" % s], 1)
-        minus(row(T.tt, s, 3), bank(b + 1), C1).then_inc(S["tV%d" % s], 1)
-        g.scalar.wait_ge(S["za%d" % s], 1)
-        g.scalar.activation(row(T.tt, s, 0), bank(b), relu, scale=C1).then_inc(S["tA%d" % s], 1)
-        g.scalar.activation(row(T.tt, s, 1), bank(b), relu, scale=-C1).then_inc(S["tA%d" % s], 1)
-        tile_done(g.vector, s)
-        quantise("t", col(s), T.tt[:, col(s, 4 * NC)], "qt%d" % s)
-        if s == 0:
+            minus(row(T.tt, s, 3), bank(b + 1), C1).then_inc(S["tV%d" % s], 1)
+            g.scalar.wait_ge(S["za%d" % s], 1)
+            g.scalar.activation(row(T.tt, s, 0), bank(b), relu, scale=C1).then_inc(S["tA%d" % s], 1)
+            g.scalar.activation(row(T.tt, s, 1), bank(b), relu, scale=-C1).then_inc(S["tA%d" % s], 1)
+        for s in group:
+            tile_done(g.vector, s)
+            quantise("t", col(s), T.tt[:, col(s, 4 * NC)], "qt%d" % s)
+
+    for i in (0, 2):
+        g.scalar.wait_ge(S["sum%d" % i], 1)
+        g.scalar.activation(T.ra[:, col(i)], bank(4 + i), ident).then_inc(S["out%d" % i], 1)
+        g.vector.wait_ge(S["sum%d" % (i + 1)], 1)
+        g.vector.tensor_copy(T.ra[:, col(i + 1)], bank(5 + i)).then_inc(S["out%d" % (i + 1)], 1)
+        if i == 0:
             g.vector.wait_ge(S.ldw3, 16)
             quantise("w3", slice(0, 256), T.wb3[:], "qw3")
 
-    g.scalar.wait_ge(S.sT0, 1)
-    g.scalar.activation(T.rb[:, col(0)], bank(6), ident).then_inc(S.rb0, 1)
-    g.vector.wait_ge(S.sT1, 1)
-    g.vector.tensor_copy(T.rb[:, col(1)], bank(7)).then_inc(S.rb1, 1)
-
-    for i in range(2):
-        g.vector.wait_ge(S["own%d" % i], 1)
-        g.vector.wait_ge(S["pc%d" % i], n_far)
-        g.vector.tensor_tensor(T.sf[:, col(i)], bank(4 + i), T.pc[:, col(i)], add).then_inc(S["sf%d" % i], 1)
-    g.scalar.wait_ge(S.sf0, 1)
-    g.scalar.activation(row(T.ht, 0, 0), T.sf[:, col(0)], relu, scale=C2).then_inc(S.hA, 1)
-    g.scalar.activation(row(T.ht, 0, 1), T.sf[:, col(0)], relu, scale=-C2).then_inc(S.hA, 1)
-    g.scalar.wait_ge(S.sf1, 1)
-    g.scalar.activation(row(T.ht, 0, 2), T.sf[:, col(1)], relu, scale=C2).then_inc(S.hA, 1)
-    g.vector.wait_ge(S.sf1, 1)
-    minus(row(T.ht, 0, 3), T.sf[:, col(1)], C2).then_inc(S.hV, 1)
-    g.vector.wait_ge(S.hV, 1)
-    g.vector.wait_ge(S.hA, 3)
-    quantise("h", col(0), T.ht[:], "qh")
+    def tile_h(k):
+        g.vector.wait_ge(S["pc%d" % k], n_far)
+        for i in range(2 * k, 2 * k + 2):
+            g.vector.wait_ge(S["out%d" % i], 1)
+            g.vector.tensor_tensor(T.sf[:, col(i)], bank(4 + i), T.pc[:, col(i)], add).then_inc(S["sf%d" % i], 1)
+        a, b = 2 * k, 2 * k + 1
+        hA, hV = S["hA%d" % k], S["hV%d" % k]
+        g.scalar.wait_ge(S["sf%d" % a], 1)
+        g.scalar.activation(row(T.ht, k, 0), T.sf[:, col(a)], relu, scale=C2).then_inc(hA, 1)
+        g.scalar.activation(row(T.ht, k, 1), T.sf[:, col(a)], relu, scale=-C2).then_inc(hA, 1)
+        g.scalar.wait_ge(S["sf%d" % b], 1)
+        g.scalar.activation(row(T.ht, k, 2), T.sf[:, col(b)], relu, scale=C2).then_inc(hA, 1)
+        g.vector.wait_ge(S["sf%d" % b], 1)
+        minus(row(T.ht, k, 3), T.sf[:, col(b)], C2).then_inc(hV, 1)
+        g.vector.wait_ge(hV, 1)
+        g.vector.wait_ge(hA, 3)
+        quantise("h", col(k), T.ht[:, col(k, 4 * NC)], "qh%d" % k)
 
     g.tensor.wait_ge(S.qw3, 1)
-    g.tensor.wait_ge(S.rb0, 1)
-    g.tensor.wait_ge(S.rb1, 1)
-    for s in TILES[4:]:
+    for s in tiles[4:]:
         tile_done(g.tensor, s)
+    tile_h(1)
     for k, s in enumerate(OUTS):
-        b = (0, 2, 6)[k % 3]
-        if k >= 3:
-            g.tensor.wait_ge(S["yc%d" % OUTS[k - 3]], 2)
-        landed("h", s, "qh")
+        b = 2 * (k % 2)
+        if k >= 2:
+            g.tensor.wait_ge(S["yc%d" % OUTS[k - 2]], 2)
+        if s < 2:
+            g.tensor.wait_ge(S["qh%d" % s], 1)
+        else:
+            for e in "qs":
+                g.tensor.wait_ge(S["h%s%d" % (e, me[s])], n_split)
         for i, n in ((0, "ya"), (1, "yv")):
             mm(b + i, "w3", col(i), "h", col(s)).then_inc(S["%s%d" % (n, s)], 1)
         g.scalar.wait_ge(S["ya%d" % s], 1)
-        g.scalar.activation(T.yb[:, col(2 * s)], bank(b), ident).then_inc(S["yc%d" % s], 1)
+        g.scalar.activation(T.yb[:, col(2 * me[s])], bank(b), ident).then_inc(S["yc%d" % s], 1)
         g.vector.wait_ge(S["yv%d" % s], 1)
-        g.vector.tensor_copy(T.yb[:, col(2 * s + 1)], bank(b + 1)).then_inc(S["yc%d" % s], 1)
+        g.vector.tensor_copy(T.yb[:, col(2 * me[s] + 1)], bank(b + 1)).then_inc(S["yc%d" % s], 1)
+        if k == 0:
+            tile_h(0)

import numpy as np
from concourse.bass import DstId, RemoteDMATransfer
from concourse.mybir import dt, AluOpType, ActivationFunctionType

N = 6
NC = 128
C1 = float(np.float32(0.043))
C2 = float(np.float32(0.01755))
CODES = "float8_e4m3fn_x4"


def packed(name, n):
    return {name + "q": ("sbuf", [128, n], CODES), name + "s": ("sbuf", [128, n], "uint8")}


SCRATCH = {
    "xb": ("sbuf", [128, 4 * NC], "bfloat16"),
    "wb1": ("sbuf", [128, 1024], "bfloat16"),
    "wb2": ("sbuf", [128, 1024], "bfloat16"),
    "wb3": ("sbuf", [128, 1024], "bfloat16"),
    "tt": ("sbuf", [128, N * 4 * NC], "bfloat16"),
    "ht": ("sbuf", [128, 2 * 4 * NC], "bfloat16"),
    "ra": ("sbuf", [128, 512], "float32"),
    "pc": ("sbuf", [128, 512], "float32"),
    "sf": ("sbuf", [128, 512], "float32"),
    "yb": ("sbuf", [128, N * 256], "float32"),
    "ps": ("psum", [128, 512 * 8], "float32"),
}
SCRATCH.update(packed("w1", 256))
SCRATCH.update(packed("w2", 256))
SCRATCH.update(packed("w3", 256))
SCRATCH.update(packed("wp", 512))
SCRATCH.update(packed("x", N * NC))
SCRATCH.update(packed("t", N * NC))
SCRATCH.update(packed("u", 4 * NC))
SCRATCH.update(packed("h", N * NC))

LEFT = "xpwuvecgh"
SEMAPHORES = (["ldx", "ldw1", "ldw2", "ldw3", "qx", "qw1", "qw2", "qw3", "stored"]
              + ["left" + n for n in LEFT]
              + ["%s%d" % (n, i) for n in ("sum", "out", "sf") for i in range(4)]
              + ["%s%d" % (n, k) for n in ("pc", "hA", "hV", "qh") for k in range(2)]
              + ["%s%s%d" % (n, e, r) for n in "xhwuv" for e in "qs" for r in range(N)]
              + ["%s%d" % (n, s) for n in ("za", "zb", "tA", "tV", "qt", "ya", "yv", "yc") for s in range(N)])

GROUPS = ((0,), (4, 2), (1,), (3, 5))
OUTS = (1, 0, 3, 5, 4, 2)
STORES = "t4 >p t0 >e t2 t5 t1 >c t3 h y0 y135 >h y4 y2".split()


def rank_program(g, core, T, topo):
    rank = T.rank_of(core)
    if rank is None:
        return
    S = T.sem
    cores = T.cores

    def home(r):
        return [q for q in range(N) if topo.chip(cores[q]) == topo.chip(cores[r])]

    def twin(r):
        away = [q for q in range(N) if topo.chip(cores[q]) != topo.chip(cores[r])]
        return away[home(r).index(r)]

    def peers(r):
        h = home(r)
        k = h.index(r)
        return [h[(k + d) % len(h)] for d in range(1, len(h))]

    def slots(r):
        out = []
        for q in [r] + peers(r):
            out += [q, twin(q)]
        return out

    def slot_of(d, r):
        return slots(d).index(r)

    def dst(r):
        rid, pid, _ = topo.addr(cores[r])
        return DstId(rid=rid, pnc=pid)

    def bits(m):
        return [e for e in range(16) if (m >> e) & 1]

    me, pe, tw = slots(rank), peers(rank), twin(rank)
    away = [tw] + [r for r in range(N) if r not in home(rank) and r != tw]
    far = topo.mask(core, cores[tw])
    near = topo.mask(core, cores[pe[0]])
    rest = near & ~far
    nb = bits(near)
    split = [sum(1 << e for e in nb[0::2]), sum(1 << e for e in nb[1::2])]
    n_far, n_rest, n_split = len(bits(far)), len(bits(rest)), len(bits(split[0]))
    sent = {}

    def col(s, w=NC):
        return slice(w * s, w * (s + 1))

    def raw(name, e, sl):
        v = T[name + e][:, sl]
        return v.bitcast(dt.uint8) if e == "q" else v

    def bank(b):
        return T.ps[:, 512 * b:512 * b + NC]

    def copy(src, dsts, mask, sem):
        return RemoteDMATransfer(dst_ids=[dst(d) for d, _ in dsts], dma_engine_mask=mask, remote_sem=S[sem],
                                 srcs=[src], dsts=[a for _, a in dsts], alu_op=0)

    def call(transfers, n, what):
        g.remote_dma_fused(transfers, local_sem=S["left" + what])
        sent[what] = sent.get(what, 0) + n

    def gone(queue, what):
        queue.wait_ge(S["left" + what], sent[what])

    def to_group(n, e, group, mask):
        return copy(raw(n, e, col(0)), [(d, raw(n, e, col(slot_of(d, rank)))) for d in group], mask, "%s%s%d" % (n, e, rank))

    def to_peers(n, e, s, what):
        r = me[s]
        call([copy(raw(n, e, col(s)), [(p, raw(n, e, col(slot_of(p, r))))], split[j], "%s%s%d" % (n, e, r))
              for j, p in enumerate(pe)], 2 * n_split, what)

    def t_to_peers(off, what):
        for j in range(2):
            g.wait_ge(S["qt%d" % (2 + 2 * j + off)], 1)
        for e in "qs":
            call([copy(raw("t", e, col(2 + 2 * j + off)), [(p, raw("u", e, col(2 * peers(p).index(rank) + off)))],
                       split[j], "%s%s%d" % (what, e, rank)) for j, p in enumerate(pe)], 2 * n_split, what)

    def sum_out(k, what):
        for i in range(2):
            g.wait_ge(S["out%d" % (2 * k + i)], 1)
        call([copy(T.ra[:, col(k, 256)], [(tw, T.pc[:, col(1 - k, 256)])], far, "pc%d" % (1 - k))], n_far, what)

    g.wait_ge(S.qx, 1)
    call([to_group("x", "q", [tw], far), to_group("x", "q", pe, rest)], n_far + n_rest, "x")
    call([to_group("x", "s", away, far), to_group("x", "s", pe, rest)], n_far + n_rest, "x")
    g.wait_ge(S["xq%d" % tw], n_far)
    to_peers("x", "q", 1, "p")
    g.wait_ge(S.qw2, 1)
    for e in "qs":
        call([copy(raw("w2", e, col(0, 256)), [(p, raw("wp", e, col(peers(p).index(rank), 256)))], split[j],
                   "w%s%d" % (e, rank)) for j, p in enumerate(pe)], 2 * n_split, "w")
    t_to_peers(0, "u")
    t_to_peers(1, "v")
    sum_out(0, "e")
    sum_out(1, "c")
    for k, what in ((1, "g"), (0, "h")):
        g.wait_ge(S["qh%d" % k], 1)
        for e in "qs":
            to_peers("h", e, k, what)

    for n, b in (("x", "xb"), ("w1", "wb1"), ("w2", "wb2"), ("w3", "wb3")):
        g.sync.dma_start(T[b][:], T[n][:]).then_inc(S["ld" + n], 16)

    def tile_done(queue, s):
        queue.wait_ge(S["tA%d" % s], 2)
        queue.wait_ge(S["tV%d" % s], 2)

    def store(out, in_):
        g.sync.dma_start(out, in_).then_inc(S.stored, 16)

    for what in STORES:
        if what[0] == ">":
            gone(g.sync, what[1])
        elif what[0] == "t":
            s = int(what[1])
            tile_done(g.sync, s)
            store(T.t[me[s]], T.tt[:, col(s, 4 * NC)])
        elif what[0] == "y":
            ranks = []
            for s in what[1:]:
                g.sync.wait_ge(S["yc" + s], 2)
                ranks.append(me[int(s)])
            c = slice(256 * min(ranks), 256 * (max(ranks) + 1))
            store(T.y[:, c], T.yb[:, c])
        else:
            g.sync.wait_ge(S.hA0, 3)
            g.sync.wait_ge(S.hV0, 1)
            store(T.h[:], T.ht[:, col(0, 4 * NC)])
    g.sync.wait_ge(S.stored, 16 * len([w for w in STORES if w[0] != ">"]))
    for k in LEFT:
        gone(g, k)

    relu, ident, add = ActivationFunctionType.Relu, ActivationFunctionType.Copy, AluOpType.add

    def plus(out, src, c):
        return g.vector.tensor_scalar(out, src, 0.0, c, AluOpType.max, AluOpType.mult)

    def minus(out, src, c):
        return g.vector.tensor_scalar(out, src, -c, 0.0, AluOpType.mult, AluOpType.max)

    def row(buf, s, b):
        return buf[:, 4 * NC * s + b:4 * NC * (s + 1):4]

    def pair(name, sl):
        return T[name + "q"][:, sl], T[name + "s"][:, sl]

    def mm(b, w, wsl, x, xsl, start=True, stop=True):
        wq, wsc = pair(w, wsl)
        xq, xsc = pair(x, xsl)
        return g.tensor.matmul_mx(bank(b), wq, wsc, xq, xsc, start, stop)

    def quantise(name, sl, tile, sem):
        q, sc = pair(name, sl)
        g.vector.quantize_mx(q, sc, tile).then_inc(S[sem], 1)

    tiles = [s for group in GROUPS for s in group]

    def x_landed(s):
        if s == 0:
            g.tensor.wait_ge(S.qx, 1)
            return
        g.tensor.wait_ge(S["xq%d" % me[s]], n_rest if s % 2 == 0 else n_far if s == 1 else n_split)
        g.tensor.wait_ge(S["xs%d" % me[s]], n_far if s % 2 else n_rest)

    def own_term(k):
        g.tensor.wait_ge(S.qw2, 1)
        g.tensor.wait_ge(S["qt%d" % k], 1)
        tile_done(g.tensor, tiles[2 + k])
        for i in range(2):
            mm(4 + 2 * k + i, "w2", col(i), "t", col(k), True, False)

    g.tensor.wait_ge(S.qw1, 1)
    for k, s in enumerate(tiles):
        if k >= 4:
            tile_done(g.tensor, tiles[k - 4])
        x_landed(s)
        for i in range(2):
            mm(2 * (k % 4) + i, "w1", col(i), "x", col(s)).then_inc(S["%s%d" % (("za", "zb")[i], s)], 1)
        if k == 3:
            own_term(0)
    for k, n in ((0, "u"), (1, "v")):
        if k:
            own_term(1)
        for j in (1, 0):
            if k == 0:
                for e in "qs":
                    g.tensor.wait_ge(S["w%s%d" % (e, pe[j])], n_split)
            for e in "qs":
                g.tensor.wait_ge(S["%s%s%d" % (n, e, pe[j])], n_split)
            for i in range(2):
                op = mm(4 + 2 * k + i, "wp", col(2 * j + i), "u", col(2 * j + k), False, j == 0)
                if j == 0:
                    op.then_inc(S["sum%d" % (2 * k + i)], 1)

    for n, b in (("x", "xb"), ("w1", "wb1"), ("w2", "wb2")):
        g.vector.wait_ge(S["ld" + n], 16)
        quantise(n, slice(0, NC if n == "x" else 256), T[b][:], "q" + n)
    for group in GROUPS:
        for s in group:
            b = 2 * (tiles.index(s) % 4)
            g.vector.wait_ge(S["zb%d" % s], 1)
            plus(row(T.tt, s, 2), bank(b + 1), C1).then_inc(S["tV%d" % s], 1)
            minus(row(T.tt, s, 3), bank(b + 1), C1).then_inc(S["tV%d" % s], 1)
            g.scalar.wait_ge(S["za%d" % s], 1)
            g.scalar.activation(row(T.tt, s, 0), bank(b), relu, scale=C1).then_inc(S["tA%d" % s], 1)
            g.scalar.activation(row(T.tt, s, 1), bank(b), relu, scale=-C1).then_inc(S["tA%d" % s], 1)
        for s in group:
            tile_done(g.vector, s)
            quantise("t", col(s), T.tt[:, col(s, 4 * NC)], "qt%d" % s)

    for i in (0, 2):
        g.scalar.wait_ge(S["sum%d" % i], 1)
        g.scalar.activation(T.ra[:, col(i)], bank(4 + i), ident).then_inc(S["out%d" % i], 1)
        g.vector.wait_ge(S["sum%d" % (i + 1)], 1)
        g.vector.tensor_copy(T.ra[:, col(i + 1)], bank(5 + i)).then_inc(S["out%d" % (i + 1)], 1)
        if i == 0:
            g.vector.wait_ge(S.ldw3, 16)
            quantise("w3", slice(0, 256), T.wb3[:], "qw3")

    def tile_h(k):
        g.vector.wait_ge(S["pc%d" % k], n_far)
        for i in range(2 * k, 2 * k + 2):
            g.vector.wait_ge(S["out%d" % i], 1)
            g.vector.tensor_tensor(T.sf[:, col(i)], bank(4 + i), T.pc[:, col(i)], add).then_inc(S["sf%d" % i], 1)
        a, b = 2 * k, 2 * k + 1
        hA, hV = S["hA%d" % k], S["hV%d" % k]
        g.scalar.wait_ge(S["sf%d" % a], 1)
        g.scalar.activation(row(T.ht, k, 0), T.sf[:, col(a)], relu, scale=C2).then_inc(hA, 1)
        g.scalar.activation(row(T.ht, k, 1), T.sf[:, col(a)], relu, scale=-C2).then_inc(hA, 1)
        g.scalar.wait_ge(S["sf%d" % b], 1)
        g.scalar.activation(row(T.ht, k, 2), T.sf[:, col(b)], relu, scale=C2).then_inc(hA, 1)
        g.vector.wait_ge(S["sf%d" % b], 1)
        minus(row(T.ht, k, 3), T.sf[:, col(b)], C2).then_inc(hV, 1)
        g.vector.wait_ge(hV, 1)
        g.vector.wait_ge(hA, 3)
        quantise("h", col(k), T.ht[:, col(k, 4 * NC)], "qh%d" % k)

    g.tensor.wait_ge(S.qw3, 1)
    for s in tiles[4:]:
        tile_done(g.tensor, s)
    tile_h(1)
    for k, s in enumerate(OUTS):
        b = 2 * (k % 2)
        if k >= 2:
            g.tensor.wait_ge(S["yc%d" % OUTS[k - 2]], 2)
        if s < 2:
            g.tensor.wait_ge(S["qh%d" % s], 1)
        else:
            for e in "qs":
                g.tensor.wait_ge(S["h%s%d" % (e, me[s])], n_split)
        for i, n in ((0, "ya"), (1, "yv")):
            mm(b + i, "w3", col(i), "h", col(s)).then_inc(S["%s%d" % (n, s)], 1)
        g.scalar.wait_ge(S["ya%d" % s], 1)
        g.scalar.activation(T.yb[:, col(2 * me[s])], bank(b), ident).then_inc(S["yc%d" % s], 1)
        g.vector.wait_ge(S["yv%d" % s], 1)
        g.vector.tensor_copy(T.yb[:, col(2 * me[s] + 1)], bank(b + 1)).then_inc(S["yc%d" % s], 1)
        if k == 0:
            tile_h(0)
